import numpy as np
import ml_dtypes


def mxq(x, axis, fmt="e4m3"):
    dtype, down = {"e4m3": (ml_dtypes.float8_e4m3fn, 7), "e5m2": (ml_dtypes.float8_e5m2, 14)}[fmt]
    v = np.moveaxis(np.asarray(x, np.float32).astype(ml_dtypes.bfloat16).astype(np.float64), axis, -1)
    blocks = v.reshape(v.shape[:-1] + (-1, 32))
    amax = np.abs(blocks).max(-1, keepdims=True)
    byte = np.maximum(np.where(amax > 0, np.frexp(amax)[1] - 1 + 127, 0) - down, 1)
    scale = np.exp2(byte - 127.0)
    codes = (blocks / scale).astype(np.float32).astype(dtype).astype(np.float64)
    return np.moveaxis((codes * scale).reshape(v.shape), -1, axis)


WIDE = False


def mx_kscale(k):
    if not WIDE:
        return np.ones(k)
    levels = np.array([10, -10, 5, -5, 0])
    if k % 512:
        return np.exp2(np.random.permutation(np.resize(levels, k // 32))).repeat(32)
    a = np.empty((k // 512, 16))
    for p in range(k // 512):
        a[p, :8] = np.random.permutation(np.resize(levels, 8))
        for g in range(8):
            far = levels[np.abs(levels - a[p, g]) >= 10]
            a[p, g + 8] = far[np.random.randint(len(far))]
    return np.exp2(a.ravel()).repeat(32)


def f64(x):
    return np.asarray(x).astype(np.float64)


def striped(idx):
    return np.tile(idx.reshape(-1, 16).T, (8, 1)).astype(np.uint16)


def unstriped(offs):
    return offs[:16].T.reshape(-1).astype(np.int64)


def relu(v):
    return np.maximum(v, 0.0)


K, T, E, C, H, N = 1024, 1536, 4, 128, 512, 512


def by_expert(wq, xq):
    return np.concatenate([wq[e].T @ xq[:, e * C:(e + 1) * C] for e in range(E)], axis=1)


def setup_inputs():
    n = np.random.standard_normal
    s = mx_kscale(K)[:, None]
    u = mx_kscale(H)
    return {
        "xT": (n((K, T)) * s).astype(np.float32),
        "w1": (n((E, K, H)) / np.sqrt(K) / s[None]).astype(np.float32),
        "w3": (n((E, K, H)) / np.sqrt(K) / s[None] * u[None, None, :]).astype(np.float32),
        "w2": (n((E, H, N)) / np.sqrt(H) / u[None, :, None]).astype(np.float32),
        "gate": np.tile(np.random.uniform(0.2, 1.0, E * C), (N, 1)).astype(np.float32),
        "offs": striped(np.random.permutation(T)[:E * C]),
    }


def reference(xT, w1, w3, w2, gate, offs):
    idx = unstriped(offs)
    xq = mxq(f64(xT)[:, idx], 0, "e4m3")
    h = relu(by_expert(mxq(f64(w1), 1, "e4m3"), xq))
    h = h * by_expert(mxq(f64(w3), 1, "e4m3"), xq)
    y = by_expert(mxq(f64(w2), 1, "e4m3"), mxq(h, 0, "e4m3"))
    out = np.zeros((N, T))
    out[:, idx] = f64(gate) * y
    return out

@@ -1,0 +1,173 @@
+from contextlib import ExitStack
+
+import concourse.mybir as mybir
+
+K, T, E, C, H, N = 1024, 1536, 4, 128, 512, 512
+FLOPS = 2 * E * C * (2 * K * H + H * N)
+
+F32 = mybir.dt.float32
+BF16 = mybir.dt.bfloat16
+U32 = mybir.dt.uint32
+U16 = mybir.dt.uint16
+U8 = mybir.dt.uint8
+FP8X4 = mybir.dt.float8_e4m3fn_x4
+RELU = mybir.ActivationFunctionType.Relu
+MULT = mybir.AluOpType.mult
+
+P = 128
+J = 4
+PASS = P * J
+KP = K // PASS
+SLOTS = E * C
+BLOCKS = N // P
+HALF = N // 2
+
+M_SCALAR = 96
+N_SCALAR = 512
+N_SCALAR_HALF = 256
+
+
+def tile_routed_moe_kernel(tc, xT, w1, w3, w2, gate, offs, out):
+    nc = tc.nc
+    with ExitStack() as ctx:
+        keep = ctx.enter_context(tc.tile_pool(name="keep", bufs=1))
+        raws = ctx.enter_context(tc.tile_pool(name="raws", bufs=12))
+        stage = ctx.enter_context(tc.tile_pool(name="stage", bufs=4))
+        coded = ctx.enter_context(tc.tile_pool(name="coded", bufs=4))
+        two = ctx.enter_context(tc.tile_pool(name="two", bufs=2))
+        psum = ctx.enter_context(tc.psum_pool(name="psum", bufs=2))
+        psum_y = ctx.enter_context(tc.psum_pool(name="psum_y", bufs=4))
+
+        offsets = keep.tile([P, SLOTS // 16], U16, name="offsets")
+        nc.sync.dma_start(offsets[:], offs)
+
+        windows = [keep.tile([P, T], F32, name=f"window{b}") for b in range(BLOCKS)]
+        for b in range(BLOCKS):
+            (nc.vector if b < 2 else nc.gpsimd).memset(windows[b][:], 0.0)
+
+        x_codes = keep.tile([P, KP, SLOTS], U32, name="x_codes", align_bytes=64)
+        x_scales = keep.tile([P, KP, SLOTS], U8, name="x_scales", align_bytes=64)
+        planes = xT.rearrange("(g p t) n -> g t p n", p=P, t=J)
+        for g in range(KP):
+            picked = two.tile([P, J, SLOTS], F32, name="picked")
+            for t in range(J):
+                raw = raws.tile([P, T], F32, name="raw", align_bytes=64)
+                nc.sync.dma_start(raw[:], planes[g, t])
+                nc.vector.tensor_copy(picked[:, t, :], raw[:].indirect(offsets[:]))
+            grouped = two.tile([P, SLOTS * J], BF16, name="x_grouped", align_bytes=64)
+            nc.scalar.copy(
+                grouped[:].rearrange("p (c i t) -> p c t i", i=4, t=J),
+                picked[:].rearrange("p t (c i) -> p c t i", i=4),
+            )
+            nc.vector.quantize_mx(out=x_codes[:, g, :].bitcast(FP8X4), scales=x_scales[:, g, :], in_=grouped[:])
+
+        def load_up(w, e, g):
+            raw = raws.tile([P, J, H], F32, name="raw", align_bytes=64)
+            nc.sync.dma_start(raw[:], w[e, g * PASS : (g + 1) * PASS, :].rearrange("(p j) c -> p j c", j=J))
+            grouped = stage.tile([P, H * J], BF16, name="grouped", align_bytes=64)
+            dst = grouped[:].rearrange("p (t m j) -> p m j t", t=J, j=J)
+            src = raw[:].rearrange("p j (m t) -> p m j t", t=J)
+            nc.scalar.copy(dst[:, :M_SCALAR], src[:, :M_SCALAR])
+            nc.vector.tensor_copy(dst[:, M_SCALAR:], src[:, M_SCALAR:])
+            return grouped
+
+        def up(w, e):
+            codes = coded.tile([P, KP, H], U32, name="up_codes", align_bytes=64)
+            scales = coded.tile([P, KP, H], U8, name="up_scales", align_bytes=64)
+            for g in range(KP):
+                grouped = load_up(w, e, g)
+                nc.vector.quantize_mx(out=codes[:, g, :].bitcast(FP8X4), scales=scales[:, g, :], in_=grouped[:])
+            return codes, scales
+
+        def project(acc, codes, scales, e):
+            slots = slice(e * C, (e + 1) * C)
+            for t in range(J):
+                cols = slice(t * P, (t + 1) * P)
+                for g in range(KP):
+                    nc.tensor.matmul_mx(
+                        out=acc[:, t, :],
+                        lhsT=codes[:, g, cols].bitcast(FP8X4),
+                        lhsT_scale=scales[:, g, cols],
+                        rhs=x_codes[:, g, slots].bitcast(FP8X4),
+                        rhs_scale=x_scales[:, g, slots],
+                        start=(g == 0),
+                        stop=(g == KP - 1),
+                    )
+
+        def hidden(e):
+            codes, scales = up(w1, e)
+            acc_a = psum.tile([P, J, C], F32, name="acc_a")
+            project(acc_a, codes, scales, e)
+            act = two.tile([P, J, C], F32, name="act")
+            nc.scalar.activation(act[:], acc_a[:], RELU)
+            codes, scales = up(w3, e)
+            acc_b = psum.tile([P, J, C], F32, name="acc_b")
+            project(acc_b, codes, scales, e)
+            h = two.tile([P, C * J], BF16, name="h", align_bytes=64)
+            nc.vector.tensor_tensor(
+                h[:].rearrange("p (c t) -> p c t", t=J),
+                act[:].rearrange("p t c -> p c t"),
+                acc_b[:].rearrange("p t c -> p c t"),
+                MULT,
+            )
+            h_codes = coded.tile([P, C], U32, name="h_codes", align_bytes=64)
+            h_scales = coded.tile([P, C], U8, name="h_scales", align_bytes=64)
+            nc.vector.quantize_mx(out=h_codes[:].bitcast(FP8X4), scales=h_scales[:], in_=h[:])
+            return h_codes, h_scales
+
+        gates = keep.tile([P, BLOCKS, SLOTS], F32, name="gates")
+        weighted = keep.tile([P, BLOCKS, SLOTS], F32, name="weighted")
+
+        def load_down(e, n0, width, n_scalar):
+            raw = raws.tile([P, J, width], F32, name="raw", align_bytes=64)
+            nc.sync.dma_start(raw[:], w2[e].rearrange("(p j) n -> p j n", j=J)[:, :, n0 : n0 + width])
+            grouped = stage.tile([P, width * J], BF16, name="grouped", align_bytes=64)
+            dst = grouped[:].rearrange("p (c i j) -> p c j i", i=4, j=J)
+            src = raw[:].rearrange("p j (c i) -> p c j i", i=4)
+            nc.scalar.copy(dst[:, : n_scalar // 4], src[:, : n_scalar // 4])
+            if n_scalar < width:
+                nc.vector.tensor_copy(dst[:, n_scalar // 4 :], src[:, n_scalar // 4 :])
+            codes = coded.tile([P, width], U32, name="down_codes", align_bytes=64)
+            scales = coded.tile([P, width], U8, name="down_scales", align_bytes=64)
+            nc.vector.quantize_mx(out=codes[:].bitcast(FP8X4), scales=scales[:], in_=grouped[:])
+            return codes, scales
+
+        def down(e, n0, width, n_scalar, h_codes, h_scales):
+            codes, scales = load_down(e, n0, width, n_scalar)
+            y = psum_y.tile([P, width // P, C], F32, name="y")
+            for b in range(width // P):
+                cols = slice(b * P, (b + 1) * P)
+                nc.tensor.matmul_mx(
+                    out=y[:, b, :],
+                    lhsT=codes[:, cols].bitcast(FP8X4),
+                    lhsT_scale=scales[:, cols],
+                    rhs=h_codes[:].bitcast(FP8X4),
+                    rhs_scale=h_scales[:],
+                    start=True,
+                    stop=True,
+                )
+            blocks = slice(n0 // P, (n0 + width) // P)
+            slots = slice(e * C, (e + 1) * C)
+            nc.vector.tensor_tensor(weighted[:, blocks, slots], y[:], gates[:, blocks, slots], MULT)
+
+        def scatter(b, first, last):
+            nc.vector.tensor_copy(
+                windows[b][:].indirect(offsets[:, first // 16 : last // 16]),
+                weighted[:, b, first:last],
+            )
+
+        h0 = hidden(0)
+        h1 = hidden(1)
+        nc.sync.dma_start(gates[:], gate.rearrange("(b p) s -> p b s", p=P))
+        down(0, 0, N, N_SCALAR, *h0)
+        down(1, 0, N, N_SCALAR, *h1)
+        for b in range(BLOCKS):
+            scatter(b, 0, 2 * C)
+        h2 = hidden(2)
+        h3 = hidden(3)
+        for n0 in range(0, N, HALF):
+            down(2, n0, HALF, N_SCALAR_HALF, *h2)
+            down(3, n0, HALF, N_SCALAR_HALF, *h3)
+            for b in range(n0 // P, (n0 + HALF) // P):
+                scatter(b, 2 * C, SLOTS)
+                nc.sync.dma_start(out[b * P : (b + 1) * P, :], windows[b][:])

@@ -21,18 +21,15 @@ KP = K // PASS
 SLOTS = E * C
 BLOCKS = N // P
 HALF = N // 2
-
-M_SCALAR = 96
-N_SCALAR = 512
-N_SCALAR_HALF = 256
+EARLY = 2 * C
 
 
 def tile_routed_moe_kernel(tc, xT, w1, w3, w2, gate, offs, out):
     nc = tc.nc
     with ExitStack() as ctx:
         keep = ctx.enter_context(tc.tile_pool(name="keep", bufs=1))
-        raws = ctx.enter_context(tc.tile_pool(name="raws", bufs=12))
-        stage = ctx.enter_context(tc.tile_pool(name="stage", bufs=4))
+        raws = ctx.enter_context(tc.tile_pool(name="raws", bufs=8))
+        stage = ctx.enter_context(tc.tile_pool(name="stage", bufs=3))
         coded = ctx.enter_context(tc.tile_pool(name="coded", bufs=4))
         two = ctx.enter_context(tc.tile_pool(name="two", bufs=2))
         psum = ctx.enter_context(tc.psum_pool(name="psum", bufs=2))
@@ -40,46 +37,65 @@ def tile_routed_moe_kernel(tc, xT, w1, w3, w2, gate, offs, out):
 
         offsets = keep.tile([P, SLOTS // 16], U16, name="offsets")
         nc.sync.dma_start(offsets[:], offs)
-
         windows = [keep.tile([P, T], F32, name=f"window{b}") for b in range(BLOCKS)]
         for b in range(BLOCKS):
             (nc.vector if b < 2 else nc.gpsimd).memset(windows[b][:], 0.0)
-
+        gates = [keep.tile([P, SLOTS], F32, name=f"gate{b}") for b in range(BLOCKS)]
+        summed = keep.tile([P, BLOCKS, SLOTS], F32, name="summed")
         x_codes = keep.tile([P, KP, SLOTS], U32, name="x_codes", align_bytes=64)
         x_scales = keep.tile([P, KP, SLOTS], U8, name="x_scales", align_bytes=64)
-        planes = xT.rearrange("(g p t) n -> g t p n", p=P, t=J)
-        for g in range(KP):
-            picked = two.tile([P, J, SLOTS], F32, name="picked")
-            for t in range(J):
-                raw = raws.tile([P, T], F32, name="raw", align_bytes=64)
-                nc.sync.dma_start(raw[:], planes[g, t])
-                nc.vector.tensor_copy(picked[:, t, :], raw[:].indirect(offsets[:]))
-            grouped = two.tile([P, SLOTS * J], BF16, name="x_grouped", align_bytes=64)
-            nc.scalar.copy(
-                grouped[:].rearrange("p (c i t) -> p c t i", i=4, t=J),
-                picked[:].rearrange("p t (c i) -> p c t i", i=4),
-            )
-            nc.vector.quantize_mx(out=x_codes[:, g, :].bitcast(FP8X4), scales=x_scales[:, g, :], in_=grouped[:])
 
-        def load_up(w, e, g):
+        state = {}
+        agenda = {}
+
+        def later(step, action):
+            agenda.setdefault(step, []).append(action)
+
+        def start_x(step, g, t):
+            if t == 0:
+                state["picked", g] = two.tile([P, J, SLOTS], F32, name="picked")
+            picked = state["picked", g]
+            raw = raws.tile([P, T], F32, name="raw", align_bytes=64)
+            nc.sync.dma_start(raw[:], xT.rearrange("(g p t) n -> g t p n", p=P, t=J)[g, t])
+            nc.vector.tensor_copy(picked[:, t, :], raw[:].indirect(offsets[:]))
+            if t == J - 1:
+                grouped = two.tile([P, SLOTS * J], BF16, name="x_grouped", align_bytes=64)
+                nc.scalar.copy(
+                    grouped[:].rearrange("p (c i t) -> p c t i", i=4, t=J),
+                    picked[:].rearrange("p t (c i) -> p c t i", i=4),
+                )
+                later(
+                    step + 1,
+                    lambda: nc.vector.quantize_mx(
+                        out=x_codes[:, g, :].bitcast(FP8X4), scales=x_scales[:, g, :], in_=grouped[:]
+                    ),
+                )
+
+        def start_up(step, which, e, g):
+            w = w1 if which == 1 else w3
+            n = 64 if (which, e, g) == (3, 3, 1) else [80,64,96,128][e]
             raw = raws.tile([P, J, H], F32, name="raw", align_bytes=64)
             nc.sync.dma_start(raw[:], w[e, g * PASS : (g + 1) * PASS, :].rearrange("(p j) c -> p j c", j=J))
             grouped = stage.tile([P, H * J], BF16, name="grouped", align_bytes=64)
             dst = grouped[:].rearrange("p (t m j) -> p m j t", t=J, j=J)
             src = raw[:].rearrange("p j (m t) -> p m j t", t=J)
-            nc.scalar.copy(dst[:, :M_SCALAR], src[:, :M_SCALAR])
-            nc.vector.tensor_copy(dst[:, M_SCALAR:], src[:, M_SCALAR:])
-            return grouped
+            nc.scalar.copy(dst[:, :n], src[:, :n])
+            if n < P:
+                nc.vector.tensor_copy(dst[:, n:], src[:, n:])
+            if g == 0:
+                state["codes", which, e] = coded.tile([P, KP, H], U32, name="up_codes", align_bytes=64)
+                state["scales", which, e] = coded.tile([P, KP, H], U8, name="up_scales", align_bytes=64)
 
-        def up(w, e):
-            codes = coded.tile([P, KP, H], U32, name="up_codes", align_bytes=64)
-            scales = coded.tile([P, KP, H], U8, name="up_scales", align_bytes=64)
-            for g in range(KP):
-                grouped = load_up(w, e, g)
+            def finish():
+                codes, scales = state["codes", which, e], state["scales", which, e]
                 nc.vector.quantize_mx(out=codes[:, g, :].bitcast(FP8X4), scales=scales[:, g, :], in_=grouped[:])
-            return codes, scales
+                if g == KP - 1:
+                    project(step + 1, which, e, codes, scales)
 
-        def project(acc, codes, scales, e):
+            later(step + 1, finish)
+
+        def project(step, which, e, codes, scales):
+            acc = psum.tile([P, J, C], F32, name="acc1" if which == 1 else "acc3")
             slots = slice(e * C, (e + 1) * C)
             for t in range(J):
                 cols = slice(t * P, (t + 1) * P)
@@ -93,47 +109,57 @@ def tile_routed_moe_kernel(tc, xT, w1, w3, w2, gate, offs, out):
                         start=(g == 0),
                         stop=(g == KP - 1),
                     )
+            if which == 1:
+                act = two.tile([P, J, C], F32, name="act")
+                state["act", e] = act
+                later(step + 1, lambda: nc.scalar.activation(act[:], acc[:], RELU))
+            else:
+                later(step + 2, lambda: gated(step + 2, e, acc))
 
-        def hidden(e):
-            codes, scales = up(w1, e)
-            acc_a = psum.tile([P, J, C], F32, name="acc_a")
-            project(acc_a, codes, scales, e)
-            act = two.tile([P, J, C], F32, name="act")
-            nc.scalar.activation(act[:], acc_a[:], RELU)
-            codes, scales = up(w3, e)
-            acc_b = psum.tile([P, J, C], F32, name="acc_b")
-            project(acc_b, codes, scales, e)
+        def gated(step, e, acc):
             h = two.tile([P, C * J], BF16, name="h", align_bytes=64)
             nc.vector.tensor_tensor(
                 h[:].rearrange("p (c t) -> p c t", t=J),
-                act[:].rearrange("p t c -> p c t"),
-                acc_b[:].rearrange("p t c -> p c t"),
+                state["act", e][:].rearrange("p t c -> p c t"),
+                acc[:].rearrange("p t c -> p c t"),
                 MULT,
             )
-            h_codes = coded.tile([P, C], U32, name="h_codes", align_bytes=64)
-            h_scales = coded.tile([P, C], U8, name="h_scales", align_bytes=64)
-            nc.vector.quantize_mx(out=h_codes[:].bitcast(FP8X4), scales=h_scales[:], in_=h[:])
-            return h_codes, h_scales
 
-        gates = keep.tile([P, BLOCKS, SLOTS], F32, name="gates")
-        weighted = keep.tile([P, BLOCKS, SLOTS], F32, name="weighted")
+            def finish():
+                h_codes = coded.tile([P, C], U32, name="h_codes", align_bytes=64)
+                h_scales = coded.tile([P, C], U8, name="h_scales", align_bytes=64)
+                nc.vector.quantize_mx(out=h_codes[:].bitcast(FP8X4), scales=h_scales[:], in_=h[:])
+                state["h", e] = (h_codes, h_scales)
+                for action in state.get(("waiting", e), []):
+                    action()
 
-        def load_down(e, n0, width, n_scalar):
+            later(step + 1, finish)
+
+        def start_down(step, e, n0, width):
+            n = 448 if width == N else 160
             raw = raws.tile([P, J, width], F32, name="raw", align_bytes=64)
             nc.sync.dma_start(raw[:], w2[e].rearrange("(p j) n -> p j n", j=J)[:, :, n0 : n0 + width])
             grouped = stage.tile([P, width * J], BF16, name="grouped", align_bytes=64)
             dst = grouped[:].rearrange("p (c i j) -> p c j i", i=4, j=J)
             src = raw[:].rearrange("p j (c i) -> p c j i", i=4)
-            nc.scalar.copy(dst[:, : n_scalar // 4], src[:, : n_scalar // 4])
-            if n_scalar < width:
-                nc.vector.tensor_copy(dst[:, n_scalar // 4 :], src[:, n_scalar // 4 :])
-            codes = coded.tile([P, width], U32, name="down_codes", align_bytes=64)
-            scales = coded.tile([P, width], U8, name="down_scales", align_bytes=64)
-            nc.vector.quantize_mx(out=codes[:].bitcast(FP8X4), scales=scales[:], in_=grouped[:])
-            return codes, scales
+            nc.scalar.copy(dst[:, : n // 4], src[:, : n // 4])
+            if n < width:
+                nc.vector.tensor_copy(dst[:, n // 4 :], src[:, n // 4 :])
 
-        def down(e, n0, width, n_scalar, h_codes, h_scales):
-            codes, scales = load_down(e, n0, width, n_scalar)
+            def finish():
+                codes = coded.tile([P, width], U32, name="down_codes", align_bytes=64)
+                scales = coded.tile([P, width], U8, name="down_scales", align_bytes=64)
+                nc.vector.quantize_mx(out=codes[:].bitcast(FP8X4), scales=scales[:], in_=grouped[:])
+                action = lambda: multiply_down(e, n0, width, codes, scales)
+                if ("h", e) in state:
+                    action()
+                else:
+                    state.setdefault(("waiting", e), []).append(action)
+
+            later(step + 1, finish)
+
+        def multiply_down(e, n0, width, codes, scales):
+            h_codes, h_scales = state["h", e]
             y = psum_y.tile([P, width // P, C], F32, name="y")
             for b in range(width // P):
                 cols = slice(b * P, (b + 1) * P)
@@ -146,28 +172,36 @@ def tile_routed_moe_kernel(tc, xT, w1, w3, w2, gate, offs, out):
                     start=True,
                     stop=True,
                 )
-            blocks = slice(n0 // P, (n0 + width) // P)
-            slots = slice(e * C, (e + 1) * C)
-            nc.vector.tensor_tensor(weighted[:, blocks, slots], y[:], gates[:, blocks, slots], MULT)
+            nc.scalar.copy(summed[:, n0 // P : (n0 + width) // P, e * C : (e + 1) * C], y[:])
+            state["y", n0] = state.get(("y", n0), 0) + (e >= 2)
+            if state["y", n0] == 2:
+                for b in range(n0 // P, (n0 + width) // P):
+                    scatter(b, EARLY, SLOTS)
+                    nc.sync.dma_start(out[b * P : (b + 1) * P, :], windows[b][:])
 
         def scatter(b, first, last):
-            nc.vector.tensor_copy(
+            nc.vector.tensor_tensor(
                 windows[b][:].indirect(offsets[:, first // 16 : last // 16]),
-                weighted[:, b, first:last],
+                summed[:, b, first:last],
+                gates[b][:, first:last],
+                MULT,
             )
 
-        h0 = hidden(0)
-        h1 = hidden(1)
-        nc.sync.dma_start(gates[:], gate.rearrange("(b p) s -> p b s", p=P))
-        down(0, 0, N, N_SCALAR, *h0)
-        down(1, 0, N, N_SCALAR, *h1)
-        for b in range(BLOCKS):
-            scatter(b, 0, 2 * C)
-        h2 = hidden(2)
-        h3 = hidden(3)
-        for n0 in range(0, N, HALF):
-            down(2, n0, HALF, N_SCALAR_HALF, *h2)
-            down(3, n0, HALF, N_SCALAR_HALF, *h3)
-            for b in range(n0 // P, (n0 + HALF) // P):
-                scatter(b, 2 * C, SLOTS)
-                nc.sync.dma_start(out[b * P : (b + 1) * P, :], windows[b][:])
+        tokens = [("x", (g, t)) for g in range(KP) for t in range(J)]
+        ups = [[("up", (which, e, g)) for which in (1, 3) for g in range(KP)] for e in range(E)]
+        halves = [("down", (e, n0, HALF)) for n0 in (0, HALF) for e in (2, 3)]
+        gs = [("gate", (b,)) for b in range(BLOCKS)]
+        pieces = tokens + ups[0] + [("down", (0, 0, N)), ("down", (1, 0, N))] + ups[1] + gs[:1] + ups[2][:2] + gs[1:2] + ups[2][2:] + gs[2:3] + ups[3][:1] + gs[3:] + ups[3][1:] + halves
+        step = 0
+        for kind, args in pieces + [("none", ())] * 8:
+            if kind == "gate":
+                (b,) = args
+                nc.sync.dma_start(gates[b][:], gate[b * P : (b + 1) * P, :])
+                continue
+            if kind != "none":
+                {"x": start_x, "up": start_up, "down": start_down}[kind](step, *args)
+            for action in agenda.get(step, []):
+                action()
+            if step >= 23 and step < 27:
+                scatter(step - 23, 0, EARLY)
+            step += 1

@@ -29,7 +29,7 @@ def tile_routed_moe_kernel(tc, xT, w1, w3, w2, gate, offs, out):
     with ExitStack() as ctx:
         keep = ctx.enter_context(tc.tile_pool(name="keep", bufs=1))
         raws = ctx.enter_context(tc.tile_pool(name="raws", bufs=8))
-        stage = ctx.enter_context(tc.tile_pool(name="stage", bufs=3))
+        stage = ctx.enter_context(tc.tile_pool(name="stage", bufs=4))
         coded = ctx.enter_context(tc.tile_pool(name="coded", bufs=4))
         two = ctx.enter_context(tc.tile_pool(name="two", bufs=2))
         psum = ctx.enter_context(tc.psum_pool(name="psum", bufs=2))
@@ -40,7 +40,8 @@ def tile_routed_moe_kernel(tc, xT, w1, w3, w2, gate, offs, out):
         windows = [keep.tile([P, T], F32, name=f"window{b}") for b in range(BLOCKS)]
         for b in range(BLOCKS):
             (nc.vector if b < 2 else nc.gpsimd).memset(windows[b][:], 0.0)
-        gates = [keep.tile([P, SLOTS], F32, name=f"gate{b}") for b in range(BLOCKS)]
+        early_gates = [keep.tile([P, EARLY], F32, name=f"early_gate{b}") for b in range(BLOCKS)]
+        late_gates = [keep.tile([P, 2, SLOTS - EARLY], F32, name=f"late_gate{i}") for i in range(2)]
         summed = keep.tile([P, BLOCKS, SLOTS], F32, name="summed")
         x_codes = keep.tile([P, KP, SLOTS], U32, name="x_codes", align_bytes=64)
         x_scales = keep.tile([P, KP, SLOTS], U8, name="x_scales", align_bytes=64)
@@ -73,7 +74,7 @@ def tile_routed_moe_kernel(tc, xT, w1, w3, w2, gate, offs, out):
 
         def start_up(step, which, e, g):
             w = w1 if which == 1 else w3
-            n = 64 if (which, e, g) == (3, 3, 1) else [80,64,96,128][e]
+            n = 64 if (which, e, g) == (3, 3, 1) else [80,80,96,112][e]
             raw = raws.tile([P, J, H], F32, name="raw", align_bytes=64)
             nc.sync.dma_start(raw[:], w[e, g * PASS : (g + 1) * PASS, :].rearrange("(p j) c -> p j c", j=J))
             grouped = stage.tile([P, H * J], BF16, name="grouped", align_bytes=64)
@@ -112,7 +113,7 @@ def tile_routed_moe_kernel(tc, xT, w1, w3, w2, gate, offs, out):
             if which == 1:
                 act = two.tile([P, J, C], F32, name="act")
                 state["act", e] = act
-                later(step + 1, lambda: nc.scalar.activation(act[:], acc[:], RELU))
+                later(step + 2, lambda: nc.scalar.activation(act[:], acc[:], RELU))
             else:
                 later(step + 2, lambda: gated(step + 2, e, acc))
 
@@ -136,7 +137,7 @@ def tile_routed_moe_kernel(tc, xT, w1, w3, w2, gate, offs, out):
             later(step + 1, finish)
 
         def start_down(step, e, n0, width):
-            n = 448 if width == N else 160
+            n = 192 if width == N else 128
             raw = raws.tile([P, J, width], F32, name="raw", align_bytes=64)
             nc.sync.dma_start(raw[:], w2[e].rearrange("(p j) n -> p j n", j=J)[:, :, n0 : n0 + width])
             grouped = stage.tile([P, width * J], BF16, name="grouped", align_bytes=64)
@@ -183,25 +184,32 @@ def tile_routed_moe_kernel(tc, xT, w1, w3, w2, gate, offs, out):
             nc.vector.tensor_tensor(
                 windows[b][:].indirect(offsets[:, first // 16 : last // 16]),
                 summed[:, b, first:last],
-                gates[b][:, first:last],
+                early_gates[b][:] if first == 0 else late_gates[b // 2][:, b % 2, :],
                 MULT,
             )
 
         tokens = [("x", (g, t)) for g in range(KP) for t in range(J)]
         ups = [[("up", (which, e, g)) for which in (1, 3) for g in range(KP)] for e in range(E)]
+        downs = [("down", (e, 0, N)) for e in range(2)]
         halves = [("down", (e, n0, HALF)) for n0 in (0, HALF) for e in (2, 3)]
-        gs = [("gate", (b,)) for b in range(BLOCKS)]
-        pieces = tokens + ups[0] + [("down", (0, 0, N)), ("down", (1, 0, N))] + ups[1] + gs[:1] + ups[2][:2] + gs[1:2] + ups[2][2:] + gs[2:3] + ups[3][:1] + gs[3:] + ups[3][1:] + halves
+        early = [("early gate", (b,)) for b in range(BLOCKS)]
+        late = [("late gate", (i,)) for i in range(2)]
+        pieces = tokens + ups[0] + downs + ups[1] + early[:1] + ups[2][:2] + early[1:2] + ups[2][2:] + ups[3][:1] + early[2:3] + ups[3][1:3] + early[3:] + ups[3][3:] + halves[:1] + late[:1] + halves[1:2] + late[1:] + halves[2:]
         step = 0
         for kind, args in pieces + [("none", ())] * 8:
-            if kind == "gate":
+            if kind == "early gate":
                 (b,) = args
-                nc.sync.dma_start(gates[b][:], gate[b * P : (b + 1) * P, :])
+                nc.sync.dma_start(early_gates[b][:], gate[b * P : (b + 1) * P, :EARLY])
+                continue
+            if kind == "late gate":
+                (i,) = args
+                rows = gate.rearrange("(i b p) s -> i p b s", p=P, b=2)[i]
+                nc.sync.dma_start(late_gates[i][:], rows[:, :, EARLY:])
                 continue
             if kind != "none":
                 {"x": start_x, "up": start_up, "down": start_down}[kind](step, *args)
             for action in agenda.get(step, []):
                 action()
-            if step >= 23 and step < 27:
-                scatter(step - 23, 0, EARLY)
+            if step >= 26 and step < 30:
+                scatter(step - 26, 0, EARLY)
             step += 1

@@ -23,6 +23,10 @@ BLOCKS = N // P
 HALF = N // 2
 EARLY = 2 * C
 
+UP_ON_SCALAR = (64, 64, 96, 112)
+LAST_UP_ON_SCALAR = 80
+DOWN_ON_SCALAR = (64, 64, 96, 96)
+
 
 def tile_routed_moe_kernel(tc, xT, w1, w3, w2, gate, offs, out):
     nc = tc.nc
@@ -37,66 +41,48 @@ def tile_routed_moe_kernel(tc, xT, w1, w3, w2, gate, offs, out):
 
         offsets = keep.tile([P, SLOTS // 16], U16, name="offsets")
         nc.sync.dma_start(offsets[:], offs)
+
         windows = [keep.tile([P, T], F32, name=f"window{b}") for b in range(BLOCKS)]
         for b in range(BLOCKS):
-            (nc.vector if b < 2 else nc.gpsimd).memset(windows[b][:], 0.0)
-        early_gates = [keep.tile([P, EARLY], F32, name=f"early_gate{b}") for b in range(BLOCKS)]
-        late_gates = [keep.tile([P, 2, SLOTS - EARLY], F32, name=f"late_gate{i}") for i in range(2)]
-        summed = keep.tile([P, BLOCKS, SLOTS], F32, name="summed")
+            zeroing = nc.vector if b % 2 == 0 else nc.gpsimd
+            zeroing.memset(windows[b][:], 0.0)
+        gates = [keep.tile([P, SLOTS], F32, name=f"gate{b}") for b in range(BLOCKS)]
+        sums = keep.tile([P, BLOCKS, SLOTS], F32, name="sums")
         x_codes = keep.tile([P, KP, SLOTS], U32, name="x_codes", align_bytes=64)
         x_scales = keep.tile([P, KP, SLOTS], U8, name="x_scales", align_bytes=64)
 
-        state = {}
-        agenda = {}
+        def quantise(codes, scales, grouped):
+            nc.vector.quantize_mx(out=codes.bitcast(FP8X4), scales=scales, in_=grouped)
 
-        def later(step, action):
-            agenda.setdefault(step, []).append(action)
+        def gather_tokens(g):
+            picked = two.tile([P, J, SLOTS], F32, name="picked")
+            for t in range(J):
+                plane = raws.tile([P, T], F32, name="raw", align_bytes=64)
+                nc.sync.dma_start(plane[:], xT.rearrange("(g p t) n -> g t p n", p=P, t=J)[g, t])
+                nc.vector.tensor_copy(picked[:, t, :], plane[:].indirect(offsets[:]))
+            grouped = two.tile([P, SLOTS * J], BF16, name="x_grouped", align_bytes=64)
+            nc.scalar.copy(
+                grouped[:].rearrange("p (s i t) -> p s t i", i=4, t=J),
+                picked[:].rearrange("p t (s i) -> p s t i", i=4),
+            )
+            quantise(x_codes[:, g, :], x_scales[:, g, :], grouped[:])
 
-        def start_x(step, g, t):
-            if t == 0:
-                state["picked", g] = two.tile([P, J, SLOTS], F32, name="picked")
-            picked = state["picked", g]
-            raw = raws.tile([P, T], F32, name="raw", align_bytes=64)
-            nc.sync.dma_start(raw[:], xT.rearrange("(g p t) n -> g t p n", p=P, t=J)[g, t])
-            nc.vector.tensor_copy(picked[:, t, :], raw[:].indirect(offsets[:]))
-            if t == J - 1:
-                grouped = two.tile([P, SLOTS * J], BF16, name="x_grouped", align_bytes=64)
-                nc.scalar.copy(
-                    grouped[:].rearrange("p (c i t) -> p c t i", i=4, t=J),
-                    picked[:].rearrange("p t (c i) -> p c t i", i=4),
-                )
-                later(
-                    step + 1,
-                    lambda: nc.vector.quantize_mx(
-                        out=x_codes[:, g, :].bitcast(FP8X4), scales=x_scales[:, g, :], in_=grouped[:]
-                    ),
-                )
+        def shared_cast(dst, src, on_scalar):
+            nc.scalar.copy(dst[:, :on_scalar], src[:, :on_scalar])
+            nc.vector.tensor_copy(dst[:, on_scalar:], src[:, on_scalar:])
 
-        def start_up(step, which, e, g):
-            w = w1 if which == 1 else w3
-            n = 64 if (which, e, g) == (3, 3, 1) else [80,80,96,112][e]
+        def load_up(w, e, g, on_scalar, codes, scales):
             raw = raws.tile([P, J, H], F32, name="raw", align_bytes=64)
             nc.sync.dma_start(raw[:], w[e, g * PASS : (g + 1) * PASS, :].rearrange("(p j) c -> p j c", j=J))
             grouped = stage.tile([P, H * J], BF16, name="grouped", align_bytes=64)
-            dst = grouped[:].rearrange("p (t m j) -> p m j t", t=J, j=J)
-            src = raw[:].rearrange("p j (m t) -> p m j t", t=J)
-            nc.scalar.copy(dst[:, :n], src[:, :n])
-            if n < P:
-                nc.vector.tensor_copy(dst[:, n:], src[:, n:])
-            if g == 0:
-                state["codes", which, e] = coded.tile([P, KP, H], U32, name="up_codes", align_bytes=64)
-                state["scales", which, e] = coded.tile([P, KP, H], U8, name="up_scales", align_bytes=64)
+            shared_cast(
+                grouped[:].rearrange("p (t m j) -> p m j t", t=J, j=J),
+                raw[:].rearrange("p j (m t) -> p m j t", t=J),
+                on_scalar,
+            )
+            quantise(codes[:, g, :], scales[:, g, :], grouped[:])
 
-            def finish():
-                codes, scales = state["codes", which, e], state["scales", which, e]
-                nc.vector.quantize_mx(out=codes[:, g, :].bitcast(FP8X4), scales=scales[:, g, :], in_=grouped[:])
-                if g == KP - 1:
-                    project(step + 1, which, e, codes, scales)
-
-            later(step + 1, finish)
-
-        def project(step, which, e, codes, scales):
-            acc = psum.tile([P, J, C], F32, name="acc1" if which == 1 else "acc3")
+        def project(e, acc, codes, scales):
             slots = slice(e * C, (e + 1) * C)
             for t in range(J):
                 cols = slice(t * P, (t + 1) * P)
@@ -110,57 +96,52 @@ def tile_routed_moe_kernel(tc, xT, w1, w3, w2, gate, offs, out):
                         start=(g == 0),
                         stop=(g == KP - 1),
                     )
-            if which == 1:
-                act = two.tile([P, J, C], F32, name="act")
-                state["act", e] = act
-                later(step + 2, lambda: nc.scalar.activation(act[:], acc[:], RELU))
-            else:
-                later(step + 2, lambda: gated(step + 2, e, acc))
 
-        def gated(step, e, acc):
+        def hidden(e):
+            accs = []
+            for i, w in enumerate((w1, w3)):
+                codes = coded.tile([P, KP, H], U32, name="up_codes", align_bytes=64)
+                scales = coded.tile([P, KP, H], U8, name="up_scales", align_bytes=64)
+                for g in range(KP):
+                    last = (e, i, g) == (E - 1, 1, KP - 1)
+                    load_up(w, e, g, LAST_UP_ON_SCALAR if last else UP_ON_SCALAR[e], codes, scales)
+                    if e >= 2 and g == 0:
+                        b = 2 * (e - 2) + i
+                        nc.sync.dma_start(gates[b][:], gate[b * P : (b + 1) * P, :])
+                        scatter(b, 0, EARLY)
+                acc = psum.tile([P, J, C], F32, name=f"acc{i}")
+                project(e, acc, codes, scales)
+                accs.append(acc)
+                if i == 0:
+                    act = two.tile([P, J, C], F32, name="act")
+                    nc.scalar.activation(act[:], acc[:], RELU)
             h = two.tile([P, C * J], BF16, name="h", align_bytes=64)
             nc.vector.tensor_tensor(
                 h[:].rearrange("p (c t) -> p c t", t=J),
-                state["act", e][:].rearrange("p t c -> p c t"),
-                acc[:].rearrange("p t c -> p c t"),
+                act[:].rearrange("p t c -> p c t"),
+                accs[1][:].rearrange("p t c -> p c t"),
                 MULT,
             )
+            h_codes = coded.tile([P, C], U32, name="h_codes", align_bytes=64)
+            h_scales = coded.tile([P, C], U8, name="h_scales", align_bytes=64)
+            quantise(h_codes[:], h_scales[:], h[:])
+            return h_codes, h_scales
 
-            def finish():
-                h_codes = coded.tile([P, C], U32, name="h_codes", align_bytes=64)
-                h_scales = coded.tile([P, C], U8, name="h_scales", align_bytes=64)
-                nc.vector.quantize_mx(out=h_codes[:].bitcast(FP8X4), scales=h_scales[:], in_=h[:])
-                state["h", e] = (h_codes, h_scales)
-                for action in state.get(("waiting", e), []):
-                    action()
-
-            later(step + 1, finish)
-
-        def start_down(step, e, n0, width):
-            n = 192 if width == N else 128
+        def load_down(e, n0, width):
             raw = raws.tile([P, J, width], F32, name="raw", align_bytes=64)
             nc.sync.dma_start(raw[:], w2[e].rearrange("(p j) n -> p j n", j=J)[:, :, n0 : n0 + width])
             grouped = stage.tile([P, width * J], BF16, name="grouped", align_bytes=64)
-            dst = grouped[:].rearrange("p (c i j) -> p c j i", i=4, j=J)
-            src = raw[:].rearrange("p j (c i) -> p c j i", i=4)
-            nc.scalar.copy(dst[:, : n // 4], src[:, : n // 4])
-            if n < width:
-                nc.vector.tensor_copy(dst[:, n // 4 :], src[:, n // 4 :])
+            shared_cast(
+                grouped[:].rearrange("p (c i j) -> p c j i", i=4, j=J),
+                raw[:].rearrange("p j (c i) -> p c j i", i=4),
+                DOWN_ON_SCALAR[e] * width // (4 * P),
+            )
+            return grouped
 
-            def finish():
-                codes = coded.tile([P, width], U32, name="down_codes", align_bytes=64)
-                scales = coded.tile([P, width], U8, name="down_scales", align_bytes=64)
-                nc.vector.quantize_mx(out=codes[:].bitcast(FP8X4), scales=scales[:], in_=grouped[:])
-                action = lambda: multiply_down(e, n0, width, codes, scales)
-                if ("h", e) in state:
-                    action()
-                else:
-                    state.setdefault(("waiting", e), []).append(action)
-
-            later(step + 1, finish)
-
-        def multiply_down(e, n0, width, codes, scales):
-            h_codes, h_scales = state["h", e]
+        def down(e, n0, width, grouped, h_codes, h_scales):
+            codes = coded.tile([P, width], U32, name="down_codes", align_bytes=64)
+            scales = coded.tile([P, width], U8, name="down_scales", align_bytes=64)
+            quantise(codes[:], scales[:], grouped[:])
             y = psum_y.tile([P, width // P, C], F32, name="y")
             for b in range(width // P):
                 cols = slice(b * P, (b + 1) * P)
@@ -173,43 +154,28 @@ def tile_routed_moe_kernel(tc, xT, w1, w3, w2, gate, offs, out):
                     start=True,
                     stop=True,
                 )
-            nc.scalar.copy(summed[:, n0 // P : (n0 + width) // P, e * C : (e + 1) * C], y[:])
-            state["y", n0] = state.get(("y", n0), 0) + (e >= 2)
-            if state["y", n0] == 2:
-                for b in range(n0 // P, (n0 + width) // P):
-                    scatter(b, EARLY, SLOTS)
-                    nc.sync.dma_start(out[b * P : (b + 1) * P, :], windows[b][:])
+            nc.scalar.copy(sums[:, n0 // P : (n0 + width) // P, e * C : (e + 1) * C], y[:])
 
-        def scatter(b, first, last):
+        def scatter(b, first, end):
             nc.vector.tensor_tensor(
-                windows[b][:].indirect(offsets[:, first // 16 : last // 16]),
-                summed[:, b, first:last],
-                early_gates[b][:] if first == 0 else late_gates[b // 2][:, b % 2, :],
+                windows[b][:].indirect(offsets[:, first // 16 : end // 16]),
+                sums[:, b, first:end],
+                gates[b][:, first:end],
                 MULT,
             )
 
-        tokens = [("x", (g, t)) for g in range(KP) for t in range(J)]
-        ups = [[("up", (which, e, g)) for which in (1, 3) for g in range(KP)] for e in range(E)]
-        downs = [("down", (e, 0, N)) for e in range(2)]
-        halves = [("down", (e, n0, HALF)) for n0 in (0, HALF) for e in (2, 3)]
-        early = [("early gate", (b,)) for b in range(BLOCKS)]
-        late = [("late gate", (i,)) for i in range(2)]
-        pieces = tokens + ups[0] + downs + ups[1] + early[:1] + ups[2][:2] + early[1:2] + ups[2][2:] + ups[3][:1] + early[2:3] + ups[3][1:3] + early[3:] + ups[3][3:] + halves[:1] + late[:1] + halves[1:2] + late[1:] + halves[2:]
-        step = 0
-        for kind, args in pieces + [("none", ())] * 8:
-            if kind == "early gate":
-                (b,) = args
-                nc.sync.dma_start(early_gates[b][:], gate[b * P : (b + 1) * P, :EARLY])
-                continue
-            if kind == "late gate":
-                (i,) = args
-                rows = gate.rearrange("(i b p) s -> i p b s", p=P, b=2)[i]
-                nc.sync.dma_start(late_gates[i][:], rows[:, :, EARLY:])
-                continue
-            if kind != "none":
-                {"x": start_x, "up": start_up, "down": start_down}[kind](step, *args)
-            for action in agenda.get(step, []):
-                action()
-            if step >= 26 and step < 30:
-                scatter(step - 26, 0, EARLY)
-            step += 1
+        for g in range(KP):
+            gather_tokens(g)
+        early_h = [hidden(0), hidden(1)]
+        for e in range(2):
+            down(e, 0, N, load_down(e, 0, N), *early_h[e])
+        late_h = [hidden(2), hidden(3)]
+
+        halves = (0, HALF)
+        grouped = [[load_down(e, n0, HALF) for e in (2, 3)] for n0 in halves]
+        for i, n0 in enumerate(halves):
+            for e in (2, 3):
+                down(e, n0, HALF, grouped[i][e - 2], *late_h[e - 2])
+            for b in range(n0 // P, (n0 + HALF) // P):
+                scatter(b, EARLY, SLOTS)
+                nc.sync.dma_start(out[b * P : (b + 1) * P, :], windows[b][:])

from contextlib import ExitStack

import concourse.mybir as mybir

K, T, E, C, H, N = 1024, 1536, 4, 128, 512, 512
FLOPS = 2 * E * C * (2 * K * H + H * N)

F32 = mybir.dt.float32
BF16 = mybir.dt.bfloat16
U32 = mybir.dt.uint32
U16 = mybir.dt.uint16
U8 = mybir.dt.uint8
FP8X4 = mybir.dt.float8_e4m3fn_x4
RELU = mybir.ActivationFunctionType.Relu
MULT = mybir.AluOpType.mult

P = 128
J = 4
PASS = P * J
KP = K // PASS
SLOTS = E * C
BLOCKS = N // P
HALF = N // 2
EARLY = 2 * C

UP_ON_SCALAR = (64, 64, 96, 112)
LAST_UP_ON_SCALAR = 80
DOWN_ON_SCALAR = (64, 64, 96, 96)


def tile_routed_moe_kernel(tc, xT, w1, w3, w2, gate, offs, out):
    nc = tc.nc
    with ExitStack() as ctx:
        keep = ctx.enter_context(tc.tile_pool(name="keep", bufs=1))
        raws = ctx.enter_context(tc.tile_pool(name="raws", bufs=8))
        stage = ctx.enter_context(tc.tile_pool(name="stage", bufs=4))
        coded = ctx.enter_context(tc.tile_pool(name="coded", bufs=4))
        two = ctx.enter_context(tc.tile_pool(name="two", bufs=2))
        psum = ctx.enter_context(tc.psum_pool(name="psum", bufs=2))
        psum_y = ctx.enter_context(tc.psum_pool(name="psum_y", bufs=4))

        offsets = keep.tile([P, SLOTS // 16], U16, name="offsets")
        nc.sync.dma_start(offsets[:], offs)

        windows = [keep.tile([P, T], F32, name=f"window{b}") for b in range(BLOCKS)]
        for b in range(BLOCKS):
            zeroing = nc.vector if b % 2 == 0 else nc.gpsimd
            zeroing.memset(windows[b][:], 0.0)
        gates = [keep.tile([P, SLOTS], F32, name=f"gate{b}") for b in range(BLOCKS)]
        sums = keep.tile([P, BLOCKS, SLOTS], F32, name="sums")
        x_codes = keep.tile([P, KP, SLOTS], U32, name="x_codes", align_bytes=64)
        x_scales = keep.tile([P, KP, SLOTS], U8, name="x_scales", align_bytes=64)

        def quantise(codes, scales, grouped):
            nc.vector.quantize_mx(out=codes.bitcast(FP8X4), scales=scales, in_=grouped)

        def gather_tokens(g):
            picked = two.tile([P, J, SLOTS], F32, name="picked")
            for t in range(J):
                plane = raws.tile([P, T], F32, name="raw", align_bytes=64)
                nc.sync.dma_start(plane[:], xT.rearrange("(g p t) n -> g t p n", p=P, t=J)[g, t])
                nc.vector.tensor_copy(picked[:, t, :], plane[:].indirect(offsets[:]))
            grouped = two.tile([P, SLOTS * J], BF16, name="x_grouped", align_bytes=64)
            nc.scalar.copy(
                grouped[:].rearrange("p (s i t) -> p s t i", i=4, t=J),
                picked[:].rearrange("p t (s i) -> p s t i", i=4),
            )
            quantise(x_codes[:, g, :], x_scales[:, g, :], grouped[:])

        def shared_cast(dst, src, on_scalar):
            nc.scalar.copy(dst[:, :on_scalar], src[:, :on_scalar])
            nc.vector.tensor_copy(dst[:, on_scalar:], src[:, on_scalar:])

        def load_up(w, e, g, on_scalar, codes, scales):
            raw = raws.tile([P, J, H], F32, name="raw", align_bytes=64)
            nc.sync.dma_start(raw[:], w[e, g * PASS : (g + 1) * PASS, :].rearrange("(p j) c -> p j c", j=J))
            grouped = stage.tile([P, H * J], BF16, name="grouped", align_bytes=64)
            shared_cast(
                grouped[:].rearrange("p (t m j) -> p m j t", t=J, j=J),
                raw[:].rearrange("p j (m t) -> p m j t", t=J),
                on_scalar,
            )
            quantise(codes[:, g, :], scales[:, g, :], grouped[:])

        def project(e, acc, codes, scales):
            slots = slice(e * C, (e + 1) * C)
            for t in range(J):
                cols = slice(t * P, (t + 1) * P)
                for g in range(KP):
                    nc.tensor.matmul_mx(
                        out=acc[:, t, :],
                        lhsT=codes[:, g, cols].bitcast(FP8X4),
                        lhsT_scale=scales[:, g, cols],
                        rhs=x_codes[:, g, slots].bitcast(FP8X4),
                        rhs_scale=x_scales[:, g, slots],
                        start=(g == 0),
                        stop=(g == KP - 1),
                    )

        def hidden(e):
            accs = []
            for i, w in enumerate((w1, w3)):
                codes = coded.tile([P, KP, H], U32, name="up_codes", align_bytes=64)
                scales = coded.tile([P, KP, H], U8, name="up_scales", align_bytes=64)
                for g in range(KP):
                    last = (e, i, g) == (E - 1, 1, KP - 1)
                    load_up(w, e, g, LAST_UP_ON_SCALAR if last else UP_ON_SCALAR[e], codes, scales)
                    if e >= 2 and g == 0:
                        b = 2 * (e - 2) + i
                        nc.sync.dma_start(gates[b][:], gate[b * P : (b + 1) * P, :])
                        scatter(b, 0, EARLY)
                acc = psum.tile([P, J, C], F32, name=f"acc{i}")
                project(e, acc, codes, scales)
                accs.append(acc)
                if i == 0:
                    act = two.tile([P, J, C], F32, name="act")
                    nc.scalar.activation(act[:], acc[:], RELU)
            h = two.tile([P, C * J], BF16, name="h", align_bytes=64)
            nc.vector.tensor_tensor(
                h[:].rearrange("p (c t) -> p c t", t=J),
                act[:].rearrange("p t c -> p c t"),
                accs[1][:].rearrange("p t c -> p c t"),
                MULT,
            )
            h_codes = coded.tile([P, C], U32, name="h_codes", align_bytes=64)
            h_scales = coded.tile([P, C], U8, name="h_scales", align_bytes=64)
            quantise(h_codes[:], h_scales[:], h[:])
            return h_codes, h_scales

        def load_down(e, n0, width):
            raw = raws.tile([P, J, width], F32, name="raw", align_bytes=64)
            nc.sync.dma_start(raw[:], w2[e].rearrange("(p j) n -> p j n", j=J)[:, :, n0 : n0 + width])
            grouped = stage.tile([P, width * J], BF16, name="grouped", align_bytes=64)
            shared_cast(
                grouped[:].rearrange("p (c i j) -> p c j i", i=4, j=J),
                raw[:].rearrange("p j (c i) -> p c j i", i=4),
                DOWN_ON_SCALAR[e] * width // (4 * P),
            )
            return grouped

        def down(e, n0, width, grouped, h_codes, h_scales):
            codes = coded.tile([P, width], U32, name="down_codes", align_bytes=64)
            scales = coded.tile([P, width], U8, name="down_scales", align_bytes=64)
            quantise(codes[:], scales[:], grouped[:])
            y = psum_y.tile([P, width // P, C], F32, name="y")
            for b in range(width // P):
                cols = slice(b * P, (b + 1) * P)
                nc.tensor.matmul_mx(
                    out=y[:, b, :],
                    lhsT=codes[:, cols].bitcast(FP8X4),
                    lhsT_scale=scales[:, cols],
                    rhs=h_codes[:].bitcast(FP8X4),
                    rhs_scale=h_scales[:],
                    start=True,
                    stop=True,
                )
            nc.scalar.copy(sums[:, n0 // P : (n0 + width) // P, e * C : (e + 1) * C], y[:])

        def scatter(b, first, end):
            nc.vector.tensor_tensor(
                windows[b][:].indirect(offsets[:, first // 16 : end // 16]),
                sums[:, b, first:end],
                gates[b][:, first:end],
                MULT,
            )

        for g in range(KP):
            gather_tokens(g)
        early_h = [hidden(0), hidden(1)]
        for e in range(2):
            down(e, 0, N, load_down(e, 0, N), *early_h[e])
        late_h = [hidden(2), hidden(3)]

        halves = (0, HALF)
        grouped = [[load_down(e, n0, HALF) for e in (2, 3)] for n0 in halves]
        for i, n0 in enumerate(halves):
            for e in (2, 3):
                down(e, n0, HALF, grouped[i][e - 2], *late_h[e - 2])
            for b in range(n0 // P, (n0 + HALF) // P):
                scatter(b, EARLY, SLOTS)
                nc.sync.dma_start(out[b * P : (b + 1) * P, :], windows[b][:])
